import numpy as np, ml_dtypes
CORES = [16,17,18,19,32,33,34,35]
N = 8
import mx_ref
BF = ml_dtypes.bfloat16
def tile(rs):
    return np.stack(rs, axis=2).reshape(128, -1).astype(BF)
def pick(q, e):
    c = np.concatenate([q[0].reshape(128, -1, 4), np.zeros((128, 1, 4), np.uint8)], axis=1); s = np.concatenate([q[1], np.ones((16, 1), np.uint8)], axis=1)
    return (np.ascontiguousarray(c[:, e].reshape(128, -1)), np.ascontiguousarray(s[:, e]))
def join(*qs):
    return (np.concatenate([q[0] for q in qs], axis=1), np.concatenate([q[1] for q in qs], axis=1))
def put(q, e, v):
    c, s = q[0].reshape(128, -1, 4).copy(), q[1].copy(); c[:, e] = v[0].reshape(128, -1, 4); s[:, e] = v[1]
    return (c.reshape(128, -1), s)
def pk(c, s):
    return (np.ascontiguousarray(c), mx_ref.live(s))
def emit(q):
    return q[0], q[1]
def packed(v, rng):
    q = [mx_ref.quantize(np.ascontiguousarray(v[r])) for r in range(N)]
    return np.stack([a for a, b in q]), np.stack([mx_ref.plane(b, rng) for a, b in q])
def values_of_codes():
    e, c = np.zeros((128, 128, 4), np.float32), np.zeros((128, 2, 4), np.uint8)
    e[np.arange(128), np.arange(128), 0] = 1
    c[:127, :, 0] = np.arange(256).reshape(2, 128).T[:127]
    return mx_ref.matmul(mx_ref.quantize(e.reshape(128, 512).astype(BF)), (c.reshape(128, 8), np.full((16, 2), 127, np.uint8))).T.reshape(-1).astype(np.float64)
CODE_VALUE, SCALE_VALUE = values_of_codes(), 2.0 ** (np.arange(256) - 127.0)
def decode(q):
    return (CODE_VALUE[q[0]].reshape(16, 8, -1, 4) * SCALE_VALUE[q[1]][:, None, :, None] + 0.0).reshape(128, -1).astype(np.float32)
def f(rng, *shape):
    return mx_ref.flush((rng.standard_normal(shape, dtype=np.float32) * np.exp2(rng.integers(-2, 3, shape[:-1] + (1,)))).astype(BF))
def wide(rng, *shape, cols=0):
    v = rng.standard_normal(shape, dtype=np.float32) * np.exp2(rng.integers(-12, 13, shape)).astype(np.float32)
    if cols: v *= np.repeat(np.exp2(rng.integers(-cols, cols + 1, shape[:-2] + (1, shape[-1] // 4))) * (rng.random(shape[:-2] + (1, shape[-1] // 4)) > 0.0625), 4, axis=-1).astype(np.float32)
    return mx_ref.flush(v.astype(BF))
C, XOR = 320, [1, 2, 4]
def big(v):
    v = v.astype(np.float32)
    v[np.abs(v) < np.float32(2.0 ** -16)] = 0
    return v.astype(BF)
def numbers_of(rng):
    return {"x": big(f(rng, N, 128, 4 * C)), "u": np.array(f(rng, N, 128, 512)), "v": np.array(f(rng, N, 128, 512))}
def layers(rng):
    return big(f(rng, N, 128, 2048)).astype(np.float32).reshape(N, 8, 16, 4, 8, 16, 4)
def weights(rng, w):
    c, s = packed(np.ascontiguousarray(w).reshape(N, 128, 2048).astype(BF), rng)
    return {"wc": c, "ws": s}
def label(rng, d, e, k):
    x, u = d["x"].reshape(N, 8, 16, C, 4), d["u"].reshape(N, 128, 128, 4)
    d["u"].reshape(N, 128, 8, 16, 4)[:, :, :, :8] = 0
    for r in range(N):
        for g in range(8):
            o, a = rng.permutation(8), np.zeros((8, C), np.float32)
            a[o] = e[r, g]
            x[r, g, :2] = a.reshape(2, 4, C).transpose(0, 2, 1).astype(BF)
            for i in range(8): u[r, 16 * g + o[i] // 4, 16 * g + i, o[i] % 4] = float(k[r])
def setup_inputs(rng):
    return {**numbers_of(rng), **weights(rng, layers(rng))}
def setup_inputs_ties(rng):
    d = numbers_of(rng)
    o = rng.permutation(N)
    h = rng.permutation(8)[:4]
    e = rng.integers(0, 3, (N, 8, 8, C))
    e[o[2]] = 1
    e[o[3], h] = 0
    k = np.ones(N)
    k[o[0]], k[o[1]] = 0, -1
    label(rng, d, e, k)
    z = (N, 8, 8, C, 4)
    a = (1.125 + 0.25 * rng.integers(0, 4, z)) * np.exp2(rng.integers(-2, 5, z))
    a[:, :, 0, :, 0] = 1.96875 * 2.0 ** 12
    a = a * rng.choice([-1.0, 1.0], z)
    a[o[3], h, 1:3] = (1.375 + 0.25 * rng.integers(0, 2, (4, 2, C, 4))) * np.exp2(rng.integers(-2, 5, (4, 1, C, 1)))
    d["x"].reshape(N, 8, 16, C, 4)[:, :, 8:] = a.astype(np.float32).astype(BF)
    u = d["u"].reshape(N, 128, 128, 4)
    for g in h:
        for i in range(8): u[o[3], 16 * g + 9 + i // 4, 16 * g + i, i % 4] = 1.0
    w = layers(rng)
    w[:, :, 8] = 0
    w[:, :, :, :, :, [0, 1, 8]] = 0
    w[:, :, :, :, :, 9:] *= np.float32(0.125)
    return {**d, **weights(rng, w)}
def setup_inputs_near(rng):
    d = numbers_of(rng)
    x = d["x"].astype(np.float32).reshape(N, 8, 16, C, 4)
    x[:, :, :2] = 0
    x[:, :, 2:8] *= np.float32(0.125)
    x[:, :, 8:] = 0
    x[:, :, 0, :, 0] = rng.choice([-1.0, 1.0], (N, 8, C))
    x[:, :, 1, :, 0] = 2.0 ** -10
    x[:, :, 8:, :, 0] = rng.integers(0, 8, (N, 8, 8, C)) * 2.0 ** -23
    x[:, :, 8:12, :, 1] = 2.0 ** -30
    x[:, :, 12:, :, 1] = rng.choice([1.0, 1.125], (N, 8, 4, C)) * 2.0 ** -30
    u = d["u"].reshape(N, 128, 128, 4)
    d["u"].reshape(N, 128, 8, 16, 4)[:, :, :, :8] = 0
    o = rng.permutation(N) % 4
    for r in range(N):
        for g in rng.permutation(8)[:4]: x[r, g, 8 + rng.integers(8), rng.integers(C), 0] = 2.0 ** 14
        for h in range(0, 128, 16):
            far = int(rng.integers(8))
            for i in range(8):
                k = 1.0 if o[r] == 0 else 2.0 ** -30
                if o[r] < 2: u[r, h:h + 2, h + i, 0] = k
                if o[r] == 2 and i == far: u[r, h + 1, h + i, 0] = -1.0
                elif o[r] < 3: u[r, h + 8 + i, h + i, 0] = k
                else: u[r, h + 8 + i, h + i, 1] = k * 1.25 if i < 4 else k * 1.125
    w = layers(rng)
    for i in (0, 1, 8, 9, 10, 11, 12, 13, 14, 15):
        w[:, :, i] = 0
        w[:, :, :, :, :, i] = 0
    return {"x": x.reshape(N, 128, 4 * C).astype(BF), "u": d["u"], "v": d["v"], **weights(rng, w)}
def setup_inputs_huge(rng):
    d = numbers_of(rng)
    o = rng.permutation(N)
    a = rng.permuted(np.tile(np.repeat([2.0 ** 29, 2.0 ** 30], 256), (N, 64, 1)), axis=2).reshape(N, 8, 8, 512)
    for r in range(N):
        if o[r] < N // 2: a[r] *= (rng.permutation(8) % 2 * 2.0 - 1.0)[:, None, None]
        else:
            for g in range(8): a[r, g] *= (rng.permutation(8) % 2 * 2.0 - 1.0)[:, None]
    d["u"].reshape(N, 128, 8, 16, 4)[:, :, :, :8] = a.reshape(N, 8, 8, 128, 4).transpose(0, 3, 1, 2, 4).astype(np.float32).astype(BF)
    d["x"] = ((0.2 + 0.5 * rng.random((N, 128, 4 * C))) * 2.0 ** 29).astype(np.float32).astype(BF)
    return {**d, **weights(rng, layers(rng) * np.float32(2.0 ** -8))}
def setup_inputs_ends(rng):
    d = numbers_of(rng)
    o = rng.permutation(N) % 4
    z, k = np.where(o % 2 == 0, 2.0 ** 30, 2.0 ** -30), np.where(o < 2, 2.0 ** 30, 2.0 ** -30)
    s = rng.choice([-1.0, 1.0], (N, 128, 4 * C))
    s[o == 0] = 1.0
    d["x"] = (s * z[:, None, None]).astype(np.float32).astype(BF)
    for n in ("u", "v"): d[n] = (rng.choice([-1.0, 1.0], (N, 128, 512)) * k[:, None, None]).astype(np.float32).astype(BF)
    counts = [[3 * C + 1, 3 * C - 1, C, C - 1, 1, 0, 0, 0], [8 * C] + [0] * 7, [C] * 8, [C + 1, C - 1] + [C] * 6]
    e, i, low = np.zeros((N, 8, 8, C)), np.arange(8)[None, :, None], {}
    for r in range(N):
        if o[r] == 0:
            m, h, j = np.insert(rng.permutation(7) + 1, 2, 0), int(rng.integers(8)), int(rng.integers(C // 4))
            c = np.zeros((8, C), int)
            c[h] = m[0]
            c[np.ix_(np.delete(np.arange(8), h), np.delete(np.arange(C), j))] = rng.permutation(np.repeat(m, np.array(counts[0]) - np.array([C, 0, 7, 0, 0, 0, 0, 0]))).reshape(7, C - 1)
            c = c.reshape(8, 1, C)
            low[r] = (h, int(m[0]), j)
        else: c = rng.permutation(np.repeat(rng.permutation(8), counts[o[r]])).reshape(8, 1, C)
        equal = (rng.permutation(8) < 4)[:, None, None] & (rng.random((8, 8, C)) < 0.5)
        e[r] = np.where((i == c) | (i > c) & equal, z[r], -z[r])
    for r in low:
        e[r, low[r][0]] = z[r]
        e[r, :, :, low[r][2]] = z[r]
    label(rng, d, e, k)
    for r in low:
        h, m = low[r][:2]
        a = d["u"].reshape(N, 8, 16, 8, 16, 4)[r]
        a[:, 2:, :, :8] = -2.0 ** 30
        a[:, :, h, :8] = -2.0 ** 30
        a[h, 2, h, m, 0] = 0
    return {**d, **weights(rng, np.zeros((N, 128, 2048), np.float32))}
def setup_inputs_spread(rng):
    d = numbers_of(rng)
    d["x"] = big(wide(rng, N, 128, 4 * C, cols=6))
    return {**d, **weights(rng, layers(rng) * np.float32(0.25))}
def check_inputs(d):
    b = []
    for k in ("x", "u", "v"):
        a = np.abs(d[k].astype(np.float32))
        if not (np.isfinite(a).all() and ((a == 0) | (a >= 2.0 ** -30) & (a <= 2.0 ** 30)).all()): b.append("a value of " + k)
    none, least, most = [emit(mx_ref.quantize(np.full((128, 16), k, np.float32).astype(BF)))[1][0, 0] for k in (0.0, 2.0 ** -30, 2.0 ** 30)]
    m, t = float(np.max(np.abs(d["x"].astype(np.float32)))), 0.0
    for r in range(N):
        if ((d["wc"][r] == 0x7F) | (d["wc"][r] == 0xFF)).any(): b.append("wc: a code that is no number")
        s = mx_ref.live(d["ws"][r])
        if ((s != none) & ((s < least) | (s > most))).any(): b.append("ws: a scale out of range")
        w = np.abs(decode(pk(d["wc"][r], d["ws"][r]))).astype(np.float64).reshape(128, 512, 4)
        t = max(t, float(np.max(np.sum(w, axis=(0, 2)))))
    if not (t == 0 or m * (1 + t * 0.015625) ** 3 <= 2.0 ** 29): b.append("m * (1 + s * 0.015625)**3 is beyond 2**29, and s isn't 0")
    return b
def sources(c):
    e, over = np.full((8, C), -1), []
    for k in range(8):
        w = np.flatnonzero(c == k)
        e[k, :min(len(w), C)] = w[:C]
        over.append(w[C:])
    e[e < 0] = np.sort(np.concatenate(over))
    return e
def reference(x, u, v, wc, ws):
    qu = [mx_ref.quantize(u[r]) for r in range(N)]
    lay = [pk(wc[r], ws[r]) for r in range(N)]
    now = [x[r] for r in range(N)]
    y, om = np.zeros((N, 128, C), np.float32), np.zeros((N, 8, C), np.float32)
    oc, osc = np.zeros((N, 128, 4 * C), np.uint8), np.zeros((N, 16, C), np.uint8)
    for a in XOR:
        kept, sent = [], []
        for r in range(N):
            q = mx_ref.quantize(now[r])
            s = mx_ref.matmul(qu[r], q).reshape(8, 16, C)[:, :8] + np.float32(0.0)
            e = sources(np.argmax(s, axis=1).T.reshape(-1))
            t = decode(q).reshape(8, 16, C, 4).transpose(0, 2, 1, 3)
            made = t[e % 8, e // 8].transpose(0, 2, 1, 3).reshape(128, 4 * C).astype(BF)
            kept.append(made[:, :2 * C])
            sent.append(mx_ref.quantize(np.ascontiguousarray(made[:, 2 * C:])))
            om[r] = e
        for r in range(N):
            z = np.concatenate([kept[r], decode(sent[r ^ a]).astype(BF)], axis=1)
            q = mx_ref.quantize(z)
            now[r] = tile([mx_ref.matmul(pick(lay[r], np.arange(128 * b, 128 * b + 128)), q) * np.float32(0.015625) + z[:, b::4].astype(np.float32) for b in range(4)])
    for r in range(N):
        q = mx_ref.quantize(now[r])
        y[r] = mx_ref.matmul(mx_ref.quantize(v[r]), q)
        oc[r], osc[r] = emit(q)
    return {"y": y, "om": om, "oc": oc, "osc": osc}

from concourse.mybir import dt, AluOpType as A, ActivationFunctionType as AF

ROUNDS = [1, 2, 4]
BIG = float(2.0 ** 75)
EC = 192
SCRATCH = {}
for _d, _l in {"bfloat16": "xt 1280 yt 1280 y64 640 ut 512 vt 512 dg 192 et 3072 on 128 la 128 lb 128 lm 1024 hu 560 tw 10240",
               "float32": "st 320 fm 320 rst 160 mk 96 zf 256 occ 8 fr 8 fb 8 wv 8 w0 8 val 320 win0 4096 win1 4096 win2 4096 "
                          "w3 20 ng 20 sv 20 cc 2 gt 20 n8 20 nn 32 omt 32 yo 320 t64 640",
               "int32": "pj 2 pk 2 gi 20", "uint16": "sl 20 gl 20"}.items():
    _l = _l.split()
    for _n, _w in zip(_l[::2], _l[1::2]):
        SCRATCH[_n] = ("sbuf", [128, int(_w)], _d)
for _n, _a, _b in (("hd", 2, 96), ("rr", 2, 96), ("sa", 2, 48), ("sb", 2, 24), ("am", 4, 96), ("am1", 4, 48), ("am2", 4, 24), ("am3", 4, 12),
                   ("gb", 16, 12), ("gb1", 8, 12), ("gb2", 4, 12), ("wm", 8, 32), ("w1", 4, 20), ("w2", 2, 20)):
    SCRATCH[_n] = ("sbuf", [128, _a, _b], "float32")
for _n in "sc cb nc fp ff rj ac pa pb pc pd t0".split():
    SCRATCH[_n] = ("sbuf", [128, 2, 12], "float32")
for _n in "pi b0 b1 b2 b3 b4".split():
    SCRATCH[_n] = ("sbuf", [128, 2, 12], "int32")
for _n, _s, _w in [("xq", "xs", 320), ("uq", "us", 128), ("vq", "vs", 128), ("wq", "wsc", 512), ("eq", "es", 4 * EC), ("lq", "lqs", 256),
                   ("hq", "hs", 140), ("zq", "zs", 160)] + [(_k + "c%d" % _t, _k + "s%d" % _t, 160) for _t in range(3) for _k in "al"]:
    SCRATCH[_n] = ("sbuf", [128, _w], "float8_e4m3fn_x4")
    SCRATCH[_s] = ("sbuf", [128, _w], "uint8")
for _t in range(8):
    SCRATCH["p%d" % _t] = ("psum", [128, 512], "float32")
SEMAPHORES = ["qv", "qt", "qa", "qp", "dx0", "dx1", "du", "dv", "dw", "dz", "rota", "rotb", "lst", "outs",
              "arr0", "arr1", "arr2", "snt0", "snt1", "snt2"]
ALL = 1 << 20


def rank_program(g, core, T, topo):
    rank = T.rank_of(core)
    if rank is None:
        return
    V, P, S, Y = g.vector, g.tensor, g.scalar, g.sync
    queue = {"v": V, "t": P, "a": S, "s": Y, "p": g}
    own = {"v": "qv", "t": "qt", "a": "qa", "p": "qp"}
    cnt, clock, snap = {}, {q: {} for q in queue}, {}
    wrote, read = {}, {}

    def rg(name, lo=0, hi=ALL, step=1):
        return (name, lo, hi, step)

    def meet(a, b):
        if a[1] >= b[2] or b[1] >= a[2]:
            return False
        return not (a[3] == b[3] and a[3] > 1 and (a[1] - b[1]) % a[3] != 0)

    def need(rd, wr):
        d = []
        for r in rd:
            d += [t for (x, t) in wrote.get(r[0], []) if meet(r, x)]
        for r in wr:
            d += [t for (x, t) in wrote.get(r[0], []) + read.get(r[0], []) if meet(r, x)]
        return d

    def wait(q, toks):
        top = {}
        for s, v in toks:
            top[s] = max(top.get(s, 0), v)
        for s in list(top):
            implied = any(o != s and snap[(o, top[o])].get(s, 0) >= top[s] for o in top)
            if not implied and clock[q].get(s, 0) < top[s]:
                queue[q].wait_ge(T.sem[s], top[s])
        for s, v in top.items():
            for o, w in snap[(s, v)].items():
                clock[q][o] = max(clock[q].get(o, 0), w)
            clock[q][s] = max(clock[q].get(s, 0), v)

    def note(tok, rd, wr):
        for r in wr:
            for tab in (wrote, read):
                tab[r[0]] = [(x, t) for (x, t) in tab.get(r[0], [])
                             if not (r[1] <= x[1] and x[2] <= r[2] and (r[3] == 1 or (r[3] == x[3] and (r[1] - x[1]) % r[3] == 0)))]
            wrote[r[0]].append((r, tok))
        for r in rd:
            read.setdefault(r[0], []).append((r, tok))

    def norm(l):
        return [rg(x) if isinstance(x, str) else x for x in l]

    def op(q, fn, rd, wr, free=()):
        rd, wr, s = norm(rd), norm(wr), own[q]
        n = cnt.get(s, 0)
        wait(q, need(rd, [r for r in wr if r[0] not in free]) + ([(s, n)] if q == "p" and n else []))
        cnt[s] = n + 1
        tok = (s, n + 1)
        snap[tok] = dict(clock[q])
        fn().then_inc(T.sem[s], 1)
        note(tok, rd, wr)

    def dmas(s, jobs):
        cnt[s] = cnt.get(s, 0) + 16 * len(jobs)
        tok, sn, done = (s, cnt[s]), None, []
        for q, o, i, rd, wr in jobs:
            rd, wr = norm(rd), norm(wr)
            wait(q, need(rd, wr))
            sn = dict(clock[q]) if sn is None else {k: min(v, sn.get(k, 0)) for k, v in clock[q].items()}
            queue[q].dma_start(o, i).then_inc(T.sem[s], 16)
            done.append((rd, wr))
        snap[tok] = sn
        for rd, wr in done:
            note(tok, rd, wr)

    def mm(bank, n, lhs, rhs, rd, start=True, stop=True):
        out = T["p%d" % bank][:, 0:n]
        op("t", lambda: P.matmul_mx(out, lhs[0], lhs[1], rhs[0], rhs[1], start, stop), rd, ["p%d" % bank],
           () if start else ("p%d" % bank,))

    pool = [0]

    def bank():
        pool[0] += 1
        return 2 + pool[0] % 6

    def tt(o, a, b, k, rd, wr):
        op("v", lambda: V.tensor_tensor(o, a, b, k), rd, wr)

    def ts(o, a, s1, s2, rd, wr, k0, k1=None):
        if k1 is None:
            op("v", lambda: V.tensor_scalar(o, a, s1, None, k0), rd, wr)
        else:
            op("v", lambda: V.tensor_scalar(o, a, s1, s2, k0, k1), rd, wr)

    def act(o, i, rd, wr, scale=1.0):
        op("a", lambda: S.activation(o, i, AF.Copy, scale=scale), rd, wr)

    def fill(ap, c, wr):
        op("v", lambda: V.memset(ap, c), [], wr)

    def quant(q, s, i, rd, wr):
        op("v", lambda: V.quantize_mx(q, s, i), rd, wr)

    dmas("dx0", [("s", T.xt[:, 0:640], T.x[:, 0:640], [], [rg("xt", 0, 640)])])
    dmas("du", [("a", T.ut[:], T.u[:], [], ["ut"])])
    dmas("dx1", [("s", T.xt[:, 640:1280], T.x[:, 640:1280], [], [rg("xt", 640, 1280)])])

    flag = {"allow_small_or_imprecise_dtypes": True}
    quarters = [(a, slice(32 * a, 32 * a + 32)) for a in range(4)]
    fill(T.dg[:], 0.0, ["dg"])
    fill(T.on[:], 1.0, ["on"])
    for b in range(4):
        fill(T.et[:, 4 * EC * b:4 * EC * (b + 1)], 0.0, [rg("et", 4 * EC * b, 4 * EC * (b + 1))])
    fill(T.hu[:], 0.0, ["hu"])
    for k in (0, 128):
        op("p", lambda: g.affine_select(T.dg[:], T.dg[:], [[-1, EC]], A.not_equal, 64.0, k, 1), ["dg"], ["dg"])
    for a, p in quarters:
        op("p", lambda: g.affine_select(T.la[p, :], T.on[p, :], [[1, 4], [4, 32]], A.is_gt, 0.0, -a, -4), ["on"], [rg("la", a, a + 1)])
    op("p", lambda: g.iota(T.zf[:], [[0, 256]], 0, 0, **flag), [], ["zf"])
    op("p", lambda: g.affine_select(T.rst[:], T.zf[:, 0:160], [[0, 10], [1, 16]], A.not_equal, -BIG, 0, 0), ["zf"], ["rst"])
    op("p", lambda: g.affine_select(T.mk[:], T.zf[:, 0:96], [[0, 8], [1, 12]], A.is_equal, 1.0, 0, 0), ["zf"], ["mk"])
    for b in range(4):
        act(T.et[:, 4 * EC * b + b:4 * EC * (b + 1):4], T.dg[:], ["dg"], [rg("et", 4 * EC * b + b, 4 * EC * (b + 1))])
    for a, p in quarters:
        op("p", lambda: g.iota(T.nc[p, :, :], [[32, 2], [8192, 12]], 64 * a + 1, 256, **flag), [], [rg("nc", a, a + 1)])
    for a, p in quarters:
        op("p", lambda: g.iota(T.val[p, :], [[1280, 2], [32, 10], [1, 16]], 2560 * a, 1, **flag), [], [rg("val", a, a + 1)])
    op("p", lambda: g.iota(T.pj[:], [[0, 2]], 0, 1), [], ["pj"])
    op("p", lambda: g.iota(T.nn[:], [[0, 32]], 0, 0, **flag), [], ["nn"])
    dmas("dz", [("s", T["win%d" % t][0:128:16, :], T.zf[:], ["zf"], ["win%d" % t]) for t in range(3)])
    dmas("dw", [("s", T.wq[:].bitcast(dt.uint8), T.wc[:], [], ["wq"]), ("s", T.wsc[:], T.ws[:], [], ["wsc"])])
    dmas("dv", [("s", T.vt[:], T.v[:], [], ["vt"])])

    U = (T.uq[:], T.us[:])
    CC = T.cc[:, 0:1]

    def xh(h):
        return (T.xq[:, 160 * h:160 * h + 160], T.xs[:, 160 * h:160 * h + 160])

    def quant_x(h):
        lo = 160 * h
        quant(xh(h)[0], xh(h)[1], T.xt[:, 4 * lo:4 * lo + 640], [rg("xt", 4 * lo, 4 * lo + 640)], [rg("xq", lo, lo + 160)])

    def choose_half(h):
        lo, hi = 160 * h, 160 * h + 160
        mm(0, 160, U, xh(h), ["uq", rg("xq", lo, hi)])
        op("v", lambda: V.transpose(T.st[:, lo:hi], T.p0[:, 0:160]), ["p0"], [rg("st", lo, hi)])
        op("v", lambda: V.tensor_tensor_scan(T.fm[:, lo:hi], T.rst[:], T.st[:, lo:hi], 0.0, A.add, A.max), ["rst", rg("st", lo, hi)], [rg("fm", lo, hi)])
        for i in range(8):
            o = 48 * (i + 1) + 20 * h
            tt(T.hu[:, o:o + 20:2], T.fm[:, lo + i:hi:16], T.fm[:, lo + 7:hi:16], A.is_ge, [rg("fm", lo, hi)], [rg("hu", o, o + 20, 2)])

    def unpack(d, lo, hi):
        for b in range(4):
            k = bank()
            e = EC * b + 16 * d
            mm(k, hi - lo, (T.eq[:, e:e + 128], T.es[:, e:e + 128]), (T.xq[:, lo:hi], T.xs[:, lo:hi]), ["eq", rg("xq", lo, hi)])
            o = 1280 * d + 320 * b
            act(T.tw[:, o + lo:o + hi], T["p%d" % k][:, 0:hi - lo], ["p%d" % k], [rg("tw", o + lo, o + hi)], 0.015625)

    def turn(s, d):
        lo, hi = 1280 * d, 1280 * (d + 2)
        dmas(s, [("s", T.tw[64 * k:64 * k + 64, 5120 + lo:5120 + hi], T.tw[64 - 64 * k:128 - 64 * k, lo:hi],
                  [rg("tw", lo, hi)], [rg("tw", 5120 + lo, 5120 + hi)]) for k in range(2)])

    for b in range(4):
        e = EC * b
        quant(T.eq[:, e:e + EC], T.es[:, e:e + EC], T.et[:, 4 * e:4 * e + 4 * EC], [rg("et", 4 * e, 4 * e + 4 * EC)], [rg("eq", e, e + EC)])
    ts(T.lb[:], T.la[:], -1.0, 1.0, ["la"], ["lb"], A.mult, A.add)
    quant(T.uq[:], T.us[:], T.ut[:], ["ut"], ["uq"])
    quant_x(0)
    quant_x(1)
    for t in (0, 2, 1, 3):
        for k in range(2):
            src = "lb" if t % 2 else "la"
            act(T.lm[:, 512 * k + t:512 * k + 512:4], T[src][:], [src], [rg("lm", 512 * k + t, 512 * k + 512, 4)], -1.0 if k else 1.0)
    choose_half(0)
    choose_half(1)
    quant(T.lq[:], T.lqs[:], T.lm[:], ["lm"], ["lq"])
    unpack(0, 0, 320)
    unpack(1, 0, 320)

    for t in range(3):
        W = T["win%d" % t]
        op("v", lambda: V.tensor_copy(T.hu[:, 5:432:2], T.hu[:, 0:427:2]), [rg("hu", 0, 432, 2)], [rg("hu", 5, 433, 2)])
        quant(T.hq[:], T.hs[:], T.hu[:], ["hu"], ["hq"])
        mm(1, 128, (T.lq[:, 0:128], T.lqs[:, 0:128]), (T.hq[:, 12:140], T.hs[:, 12:140]), ["lq", "hq"], True, False)
        mm(1, 128, (T.lq[:, 128:256], T.lqs[:, 128:256]), (T.hq[:, 0:128], T.hs[:, 0:128]), ["lq", "hq"], False, True)
        for e in range(2):
            tt(T.hd[:, e, :], T.hu[:, 48 + 2 * e:432:4], T.hu[:, 2 * e:384:4], A.subtract, [rg("hu", 0, 432, 2)], ["hd%d" % e])
        for e in range(2):
            tt(T.sa[:, e, :], T.hu[:, 48 + 2 * e:240:4], T.hu[:, 240 + 2 * e:432:4], A.add, [rg("hu", 0, 432, 2)], ["sa%d" % e])
        tt(T.sb[:], T.sa[:, :, 0:24], T.sa[:, :, 24:48], A.add, ["sa0", "sa1"], ["sb"])
        tt(T.sc[:], T.sb[:, :, 0:12], T.sb[:, :, 12:24], A.add, ["sb"], ["sc"])
        ts(T.cb[:], T.sc[:], -16384.0, 131072.0, ["sc"], ["cb"], A.mult, A.add)
        op("v", lambda: V.tensor_tensor_scan(T.rr[:, 0, :], T.mk[:], T.p1[:, 0:96], 0.0, A.mult, A.add), ["mk", "p1"], ["rr0"])
        tt(T.rr[:, 1, :], T.rr[:, 0, :], T.hd[:, 0, :], A.add, ["rr0", "hd0"], ["rr1"])
        for e in range(2):
            tt(T.am[:, e, :], T.rr[:, e, :], T.hd[:, e, :], A.mult, ["rr%d" % e, "hd%d" % e], ["am%d" % e])
            ts(T.am[:, 2 + e, :], T.rr[:, e, :], 320.0, 32.0, ["rr%d" % e], ["am%d" % (2 + e)], A.min, A.mult)
        ts(T.occ[:], T.rr[:, 0, 10:96:12], 320.0, None, ["rr0"], ["occ"], A.min)
        tt(T.am1[:], T.am[:, :, 0:48], T.am[:, :, 48:96], A.add, ["am0", "am1", "am2", "am3"], ["am_1"])
        ts(T.fr[:], T.occ[:], -32.0, 10240.0, ["occ"], ["fr"], A.mult, A.add)
        ts(T.wv[:], T.occ[:], 32.0, 6144.0, ["occ"], ["wv"], A.mult, A.add)
        ts(T.w0[:], T.occ[:], 32.0, -1.0, ["occ"], ["w0"], A.mult, A.add)
        tt(T.am2[:], T.am1[:, :, 0:24], T.am1[:, :, 24:48], A.add, ["am_1"], ["am_2"])
        op("v", lambda: V.tensor_tensor_scan(T.fb[:], T.fr[:], T.zf[:, 0:8], 1.0, A.add, A.add), ["fr", "zf"], ["fb"])
        tt(T.am3[:], T.am2[:, :, 0:12], T.am2[:, :, 12:24], A.add, ["am_2"], ["am_3"])
        CS, MS = T.am3[:, 0:2, :], T.am3[:, 2:4, :]
        tt(T.fp[:], T.nc[:], MS, A.subtract, ["nc", "am_3"], ["fp"])
        ts(T.rj[:], CS, 320.0, None, ["am_3"], ["rj"], A.is_ge)
        ts(T.pa[:], CS, 32.0, None, ["am_3"], ["pa"], A.mult)
        ts(T.ac[:], CS, 320.0, None, ["am_3"], ["ac"], A.is_lt)
        tt(T.ff[:], T.fp[:], T.rj[:], A.mult, ["fp", "rj"], ["ff"])
        tt(T.pb[:], T.pa[:], T.cb[:], A.add, ["pa", "cb"], ["pb"])
        ts(T.t0[:], T.rj[:], T.w0[:, 0:1], None, ["rj", "w0"], ["t0"], A.mult)
        for c in range(1, 8):
            ts(T.gb[:, 2 * c:2 * c + 2, :], T.ff[:], T.fb[:, c - 1:c], T.wv[:, c:c + 1], ["ff", "fb", "wv"], ["gb%d" % c], A.is_ge, A.mult)
            if c == 2:
                tt(T.pc[:], T.pb[:], T.ac[:], A.mult, ["pb", "ac"], ["pc"])
            if c == 4:
                tt(T.pd[:], T.pc[:], T.t0[:], A.add, ["pc", "t0"], ["pd"])
            if c == 6:
                tt(T.gb[:, 0:2, :], T.ff[:], T.pd[:], A.add, ["ff", "pd"], ["gb0"])
        tt(T.gb1[:], T.gb[:, 0:8, :], T.gb[:, 8:16, :], A.add, ["gb%d" % c for c in range(8)], ["gb_1"])
        tt(T.gb2[:], T.gb1[:, 0:4, :], T.gb1[:, 4:8, :], A.add, ["gb_1"], ["gb_2"])
        tt(T.pi[:], T.gb2[:, 0:2, :], T.gb2[:, 2:4, :], A.add, ["gb_2"], ["pi"])
        ts(T.b0[:], T.pi[:], 480, None, ["pi"], ["b0"], A.bitwise_and)
        ts(T.b1[:], T.pi[:], 5, 3584, ["pi"], ["b1"], A.arith_shift_right, A.bitwise_and)
        ts(T.b2[:], T.pi[:], 9, 31, ["pi"], ["b2"], A.arith_shift_right, A.bitwise_and)
        tt(T.b3[:], T.b0[:], T.b1[:], A.add, ["b0", "b1"], ["b3"])
        tt(T.b4[:], T.b3[:], T.b2[:], A.add, ["b3", "b2"], ["b4"])
        for e in range(2):
            op("v", lambda: V.tensor_copy(T.sl[:, 10 * e:10 * e + 10], T.b4[:, e, 0:10]), ["b4"], [rg("sl", 10 * e, 10 * e + 10)])
        op("v", lambda: V.tensor_copy(W[:].indirect(T.sl[:]), T.val[:]), ["sl", "val"], ["win%d" % t])
        turn("rota", 0)
        unpack(2, 0, 320)
        unpack(3, 0, 320)
        turn("rotb", 2)
        dmas("lst", [("as"[x % 2], T.wm[:, x, :], W[16 * x:16 * x + 1, :], ["win%d" % t], ["wm%d" % x]) for x in range(8)])
        if t == 0:
            quant(T.vq[:], T.vs[:], T.vt[:], ["vt"], ["vq"])
            ts(T.pk[:], T.pj[:], 4, None, ["pj"], ["pk"], A.arith_shift_right)
            ts(T.cc[:], T.pk[:], 1280.0, None, ["pk"], ["cc"], A.mult)
        tt(T.w1[:], T.wm[:, 0:4, 0:20], T.wm[:, 4:8, 0:20], A.add, ["wm%d" % x for x in range(8)], ["w1"])
        tt(T.w2[:], T.w1[:, 0:2, :], T.w1[:, 2:4, :], A.add, ["w1"], ["w2"])
        tt(T.w3[:], T.w2[:, 0, :], T.w2[:, 1, :], A.add, ["w2"], ["w3"])
        ts(T.ng[:], T.w3[:], CC, 10240.0, ["w3", "cc"], ["ng"], A.is_lt, A.mult)
        tt(T.sv[:], T.w3[:], T.ng[:], A.add, ["w3", "ng"], ["sv"])
        ts(T.gl[:], T.sv[:], CC, None, ["sv", "cc"], ["gl"], A.subtract)

        def gather(h):
            for b in (0, 2, 1, 3):
                o = T.yt[:, 640 * h + b:640 * h + 640:4]
                i = T.tw[:, 320 * b:320 * b + 9280].indirect(T.gl[:, 10 * h:10 * h + 10])
                rd, wr = ["gl", rg("tw", 320 * b, 320 * b + 9280)], [rg("yt", 640 * h + b, 640 * h + 640, 4)]
                if b < 2:
                    op("v", lambda: V.tensor_copy(o, i), rd, wr)
                else:
                    act(o, i, rd, wr)
        gather(1)
        cq, cs, lc, ls = T["ac%d" % t], T["as%d" % t], T["lc%d" % t], T["ls%d" % t]
        quant(cq[:], cs[:], T.yt[:, 640:1280], [rg("yt", 640, 1280)], ["cq%d" % t])
        dst = T.cores[rank ^ ROUNDS[t]]
        rid, pid = topo.addr(dst)[0:2]
        mask = 0
        for e in topo.engines(core, dst)[0:8]:
            mask |= 1 << e
        wait("p", need([rg("cq%d" % t)], []))
        arr, snt = T.sem["arr%d" % t], T.sem["snt%d" % t]
        g.remote_dma(lc[:].bitcast(dt.uint8), cq[:].bitcast(dt.uint8), arr, snt, pid, rid, mask)
        g.remote_dma(ls[:], cs[:], arr, snt, pid, rid, mask)
        snap[("arr%d" % t, 16)] = {}
        note(("arr%d" % t, 16), [], [rg("lc%d" % t)])
        cnt["arr%d" % t] = cnt["snt%d" % t] = 16

        gather(0)
        quant(T.zq[:], T.zs[:], T.yt[:, 0:640], [rg("yt", 0, 640)], ["zq"])
        for b in range(4):
            act(T.y64[:, b:640:4], T.yt[:, b:640:4], [rg("yt", b, 640, 4)], [rg("y64", b, 640, 4)], 64.0)
        for b in range(4):
            k = bank()
            w = (T.wq[:, 128 * b:128 * b + 128], T.wsc[:, 128 * b:128 * b + 128])
            mm(k, 160, w, (T.zq[:], T.zs[:]), ["wq", "wsc", "zq"])
            tt(T.t64[:, 160 * b:160 * b + 160], T["p%d" % k][:, 0:160], T.y64[:, b:640:4], A.add, ["p%d" % k, rg("y64", b, 640, 4)], [rg("t64", 160 * b, 160 * b + 160)])
            act(T.xt[:, b:640:4], T.t64[:, 160 * b:160 * b + 160], [rg("t64", 160 * b, 160 * b + 160)], [rg("xt", b, 640, 4)], 0.015625)
        quant_x(0)
        if t < 2:
            choose_half(0)
        else:
            mm(0, 160, (T.vq[:], T.vs[:]), xh(0), ["vq", rg("xq", 0, 160)])
            ts(T.gi[:], T.w3[:], -160.0, 0.00078125, ["w3"], ["gi"], A.add, A.mult)
            ts(T.n8[:], T.w3[:], 8.0, None, ["w3"], ["n8"], A.mult)
            act(T.yo[:, 0:160], T.p0[:, 0:160], ["p0"], [rg("yo", 0, 160)])
            ts(T.gt[:], T.gi[:], -10239.0, None, ["gi"], ["gt"], A.mult)
            tt(T.nn[:, 0:20], T.n8[:], T.gt[:], A.add, ["n8", "gt"], ["nn"])
            op("v", lambda: V.transpose(T.omt[:], T.nn[:]), ["nn"], ["omt"])
        for b in range(4):
            k = bank()
            w = (T.wq[:, 128 * b:128 * b + 128], T.wsc[:, 128 * b:128 * b + 128])
            e = EC * b
            mm(k, 160, w, (lc[:], ls[:]), ["wq", "wsc", "lc%d" % t], True, False)
            mm(k, 160, (T.eq[:, e:e + 128], T.es[:, e:e + 128]), (lc[:], ls[:]), ["eq", "lc%d" % t], False, True)
            o, i = T.xt[:, 640 + b:1280:4], T["p%d" % k][:, 0:160]
            rd, wr = ["p%d" % k], [rg("xt", 640 + b, 1280, 4)]
            if t == 2 and b % 2 == 0:
                ts(o, i, 0.015625, None, rd, wr, A.mult)
            else:
                act(o, i, rd, wr, 0.015625)
        if t < 2:
            unpack(0, 0, 160)
        quant_x(1)
        if t < 2:
            choose_half(1)
            unpack(0, 160, 320)
            unpack(1, 0, 320)

    def store_q(h, q1, q2):
        lo, hi = 160 * h, 160 * h + 160
        return [(q1, T.oc[:, 4 * lo:4 * hi], T.xq[:, lo:hi].bitcast(dt.uint8), [rg("xq", lo, hi)], [])] + \
               [(q2, T.osc[4 * k:4 * k + 4, lo:hi], T.xs[32 * k:32 * k + 4, lo:hi], [rg("xq", lo, hi)], []) for k in range(4)]

    jobs = [("s", T.om[c:c + 1, :], T.omt[32 * (c // 2):32 * (c // 2) + 20, 16 * (c % 2):16 * (c % 2) + 16], ["omt"], []) for c in range(8)]
    jobs += store_q(0, "s", "s")
    jobs += [("s", T.y[:, 0:160], T.yo[:, 0:160], [rg("yo", 0, 160)], [])]
    mm(1, 160, (T.vq[:], T.vs[:]), xh(1), ["vq", rg("xq", 160, 320)])
    op("v", lambda: V.tensor_copy(T.yo[:, 160:320], T.p1[:, 0:160]), ["p1"], [rg("yo", 160, 320)])
    jobs += store_q(1, "s", "a")
    jobs += [("s", T.y[:, 160:320], T.yo[:, 160:320], [rg("yo", 160, 320)], [])]
    dmas("outs", jobs)
    for s in SEMAPHORES:
        if cnt.get(s, 0) > clock["p"].get(s, 0):
            g.wait_ge(T.sem[s], cnt[s])
